import numpy as np
import ml_dtypes


def mxq(x, axis, fmt="e4m3"):
    dtype, down = {"e4m3": (ml_dtypes.float8_e4m3fn, 7), "e5m2": (ml_dtypes.float8_e5m2, 14)}[fmt]
    v = np.moveaxis(np.asarray(x, np.float32).astype(ml_dtypes.bfloat16).astype(np.float64), axis, -1)
    blocks = v.reshape(v.shape[:-1] + (-1, 32))
    amax = np.abs(blocks).max(-1, keepdims=True)
    byte = np.maximum(np.where(amax > 0, np.frexp(amax)[1] - 1 + 127, 0) - down, 1)
    scale = np.exp2(byte - 127.0)
    codes = (blocks / scale).astype(np.float32).astype(dtype).astype(np.float64)
    return np.moveaxis((codes * scale).reshape(v.shape), -1, axis)


WIDE = False


def mx_kscale(k):
    if not WIDE:
        return np.ones(k)
    levels = np.array([10, -10, 5, -5, 0])
    if k % 512:
        return np.exp2(np.random.permutation(np.resize(levels, k // 32))).repeat(32)
    a = np.empty((k // 512, 16))
    for p in range(k // 512):
        a[p, :8] = np.random.permutation(np.resize(levels, 8))
        for g in range(8):
            far = levels[np.abs(levels - a[p, g]) >= 10]
            a[p, g + 8] = far[np.random.randint(len(far))]
    return np.exp2(a.ravel()).repeat(32)


def f64(x):
    return np.asarray(x).astype(np.float64)


def striped(idx):
    return np.tile(idx.reshape(-1, 16).T, (8, 1)).astype(np.uint16)


def unstriped(offs):
    return offs[:16].T.reshape(-1).astype(np.int64)


E2M1 = np.array([0.0, 0.5, 1.0, 1.5, 2.0, 3.0, 4.0, 6.0, -0.0, -0.5, -1.0, -1.5, -2.0, -3.0, -4.0, -6.0])


def pack_weight(w, fmt):
    k, n = w.shape
    w = f64(np.asarray(w, np.float32).astype(ml_dtypes.bfloat16)).reshape(k // 32, 32, n)
    amax = np.abs(w).max(1)
    if fmt == "e4m3":
        byte = np.frexp(amax)[1] - 1 + 127 - 7
    else:
        mant, ex = np.frexp(amax / 6.0)
        byte = np.where(mant > 0.5, ex, ex - 1) + 127
    byte = np.clip(np.where(amax > 0, byte, 1), 1, 254)
    scaled = (w * np.exp2(127.0 - byte)[:, None, :]).reshape(k, n).astype(np.float32)
    by_word = np.ascontiguousarray(scaled.reshape(k // 512, 128, 4, n).transpose(0, 1, 3, 2))
    if fmt == "e4m3":
        words = by_word.astype(ml_dtypes.float8_e4m3fn).view(np.uint8)
    else:
        c = by_word.astype(ml_dtypes.float4_e2m1fn).view(np.uint8) & 0xF
        words = (c[..., 0::2] | (c[..., 1::2] << 4)).reshape(k // 512, 128, 2 * n)
    return np.ascontiguousarray(words), np.ascontiguousarray(byte.astype(np.uint8).reshape(k // 512, 16, n))


def unpack_weight(words, scales, fmt):
    g, _, n = scales.shape
    words = np.ascontiguousarray(words).reshape(g, 128, n, -1)
    if fmt == "e4m3":
        vals = words.view(ml_dtypes.float8_e4m3fn).astype(np.float64)
    else:
        nib = np.empty((g, 128, n, 4), np.uint8)
        nib[..., 0::2] = words & 0xF
        nib[..., 1::2] = words >> 4
        vals = E2M1[nib]
    vals = vals * np.repeat(np.exp2(scales.astype(np.float64) - 127.0), 8, axis=1)[..., None]
    return vals.transpose(0, 1, 3, 2).reshape(g * 512, n)


def sigmoid(v):
    return 1.0 / (1.0 + np.exp(-np.maximum(v, -700.0)))


K, T, E, C, H, N = 512, 1536, 8, 256, 512, 128
TOP = 4
PAD = 64


def by_expert(wq, xq):
    return np.concatenate([wq[e].T @ xq[:, e * C:(e + 1) * C] for e in range(E)], axis=1)


def setup_inputs():
    n = np.random.standard_normal
    s = mx_kscale(K)[:, None]
    u = mx_kscale(H)
    slot_token = np.empty(E * C, np.int64); pos = np.tile(E * C + np.arange(T) % PAD, (TOP, 1)); taken = np.zeros(T, np.int64)
    liked = np.random.randn(T)
    for e in np.random.permutation(E):
        free = np.flatnonzero(taken < TOP); pick = np.random.permutation(free[np.argsort(-(liked[free] + np.random.gumbel(size=free.size)))[:C]]); slot_token[e * C:(e + 1) * C] = pick
        pos[taken[pick], pick] = e * C + np.arange(C); taken[pick] += 1
    g = np.random.uniform(0.2, 0.8, (TOP, T))
    w1 = [pack_weight(m, "e2m1") for m in n((E, K, H)) / np.sqrt(K) / s[None]]
    w3 = [pack_weight(m, "e2m1") for m in n((E, K, H)) / np.sqrt(K) / s[None] * u[None, None, :]]
    w2 = [pack_weight(m, "e2m1") for m in n((E, H, N)) / np.sqrt(H) / u[None, :, None]]
    return {
        "xT": (n((K, T)) * s).astype(np.float32),
        "w1_words": np.stack([m[0] for m in w1]),
        "w1_scales": np.stack([m[1] for m in w1]),
        "w3_words": np.stack([m[0] for m in w3]),
        "w3_scales": np.stack([m[1] for m in w3]),
        "w2_words": np.stack([m[0] for m in w2]),
        "w2_scales": np.stack([m[1] for m in w2]),
        "gate": np.stack([np.tile(r, (N, 1)) for r in g]).astype(np.float32),
        "offs": striped(slot_token),
        "pos1": striped(pos[0]),
        "pos2": striped(pos[1]),
        "pos3": striped(pos[2]),
        "pos4": striped(pos[3]),
    }


def reference(xT, w1_words, w1_scales, w3_words, w3_scales, w2_words, w2_scales, gate, offs, pos1, pos2, pos3, pos4):
    idx = unstriped(offs)
    w1 = np.stack([unpack_weight(w1_words[e], w1_scales[e], "e2m1") for e in range(E)])
    w3 = np.stack([unpack_weight(w3_words[e], w3_scales[e], "e2m1") for e in range(E)])
    w2 = np.stack([unpack_weight(w2_words[e], w2_scales[e], "e2m1") for e in range(E)])
    xq = mxq(f64(xT)[:, idx], 0, "e4m3")
    h = sigmoid(by_expert(w1, xq))
    h = h * by_expert(w3, xq)
    y = by_expert(w2, mxq(h, 0, "e4m3"))
    y = np.concatenate([y, np.zeros((N, PAD))], axis=1)
    return sum(f64(gate[r]) * y[:, unstriped(p)] for r, p in enumerate((pos1, pos2, pos3, pos4)))

@@ -1,0 +1,303 @@
+from contextlib import ExitStack
+
+import concourse.mybir as mybir
+from concourse.masks import make_identity
+
+K, T, E, C, H, N = 512, 1536, 8, 256, 512, 128
+TOP = 4
+PAD = 64
+S = E * C
+FLOPS = 2 * S * (2 * K * H + H * N)
+
+F32 = mybir.dt.float32
+BF16 = mybir.dt.bfloat16
+I32 = mybir.dt.int32
+U32 = mybir.dt.uint32
+U16 = mybir.dt.uint16
+U8 = mybir.dt.uint8
+FP8X4 = mybir.dt.float8_e4m3fn_x4
+FP4X4 = mybir.dt.float4_e2m1fn_x4
+MULT = mybir.AluOpType.mult
+ADD = mybir.AluOpType.add
+SIGMOID = mybir.ActivationFunctionType.Sigmoid
+
+P = 128
+PER_COL = 16
+X_CHUNKS = ((512, 256), (512, 256), (256, 160), (256, 160))
+AHEAD = 3
+PE_CHUNKS = (512, 512, 256)
+LAST_CHUNK = 256
+
+
+def tile_moe_ecr_glu_sigmoid_kernel(
+    tc, xT, w1_words, w1_scales, w3_words, w3_scales, w2_words, w2_scales, gate, offs, pos1, pos2, pos3, pos4, out
+):
+    nc = tc.nc
+    with ExitStack() as ctx:
+        lists = ctx.enter_context(tc.tile_pool(name="lists", bufs=1))
+        keep = ctx.enter_context(tc.tile_pool(name="keep", bufs=1))
+        ring = ctx.enter_context(tc.tile_pool(name="ring", bufs=3))
+        psum = ctx.enter_context(tc.psum_pool(name="psum", bufs=2))
+
+        warm = keep.tile([P, 8], F32, name="warm")
+        warm_out = keep.tile([P, 8], F32, name="warm_out")
+        nc.vector.memset(warm[:], 0.0)
+        nc.scalar.activation(warm_out[:], warm[:], SIGMOID)
+
+        x_codes = keep.tile([P, T], U32, name="x_codes", align_bytes=64)
+        x_scales = keep.tile([P, T], U8, name="x_scales", align_bytes=64)
+        nc.gpsimd.memset(x_scales[:], 0)
+        ident = keep.tile([P, P], F32, name="ident")
+        make_identity(nc, ident[:])
+
+        w1_plane = keep.tile([P, E, H], U8, name="w1_plane", align_bytes=64)
+        w3_plane = keep.tile([P, E, H], U8, name="w3_plane", align_bytes=64)
+        w2_plane = keep.tile([P, E, N], U8, name="w2_plane", align_bytes=64)
+        for plane in (w1_plane, w3_plane, w2_plane):
+            nc.vector.memset(plane[:].bitcast(I32), 0)
+        y_all = keep.tile([P, S + PAD], F32, name="y_all")
+        nc.vector.memset(y_all[:, S:], 0.0)
+
+        offs_sb = lists.tile([P, S // PER_COL], U16, name="offs_sb")
+        nc.sync.dma_start(offs_sb[:], offs)
+
+        x_rows = xT.rearrange("(p j) t -> p j t", j=4)
+        raws = []
+        t0 = 0
+        for c, (width, on_vector) in enumerate(X_CHUNKS):
+            raw = keep.tile([P, 4, width], F32, name=f"x_raw{c}")
+            nc.sync.dma_start(raw[:], x_rows[:, :, t0 : t0 + width])
+            raws.append(raw)
+            t0 += width
+
+        w1_sb = keep.tile([P, E, 2 * H], U8, name="w1_sb", align_bytes=64)
+        w3_sb = keep.tile([P, E, 2 * H], U8, name="w3_sb", align_bytes=64)
+        w2_sb = keep.tile([P, E, 2 * N], U8, name="w2_sb", align_bytes=64)
+
+        def load_words(dst, src, e0, e1):
+            nc.sync.dma_start(
+                dst[:, e0:e1, :].bitcast(I32), src[e0:e1].rearrange("e s p c -> p (e s) c").bitcast(I32)
+            )
+
+        def load_scales(dst, src, e0, e1):
+            rows = src[e0:e1].rearrange("e s q c -> q (e s) c")
+            for quad in range(4):
+                nc.sync.dma_start(
+                    dst[32 * quad : 32 * quad + 4, e0:e1, :].bitcast(I32), rows[4 * quad : 4 * quad + 4].bitcast(I32)
+                )
+
+        load_words(w1_sb, w1_words, 0, 2)
+        load_words(w3_sb, w3_words, 0, 2)
+        load_scales(w1_plane, w1_scales, 0, 4)
+        load_scales(w3_plane, w3_scales, 0, 4)
+        load_scales(w2_plane, w2_scales, 0, E)
+        load_words(w2_sb, w2_words, 0, E)
+        load_words(w1_sb, w1_words, 2, 4)
+        load_words(w3_sb, w3_words, 2, 4)
+        load_scales(w1_plane, w1_scales, 4, E)
+        load_scales(w3_plane, w3_scales, 4, E)
+        load_words(w1_sb, w1_words, 4, E)
+        load_words(w3_sb, w3_words, 4, E)
+        pos_sb = []
+        for r, pos in enumerate((pos1, pos2, pos3, pos4)):
+            tile = lists.tile([P, T // PER_COL], U16, name=f"pos_sb{r}")
+            nc.sync.dma_start(tile[:], pos)
+            pos_sb.append(tile)
+        gate_sb = []
+        for r in range(TOP):
+            tile = keep.tile([P, T], F32, name=f"gate_sb{r}")
+            nc.sync.dma_start(tile[:], gate[r])
+            gate_sb.append(tile)
+
+        t0 = 0
+        for c, (width, on_vector) in enumerate(X_CHUNKS):
+            grouped = keep.tile([P, width, 4], BF16, name=f"x_grouped{c}", align_bytes=64)
+            nc.scalar.copy(
+                grouped[:, on_vector:, :].rearrange("p (c i) j -> p c j i", i=4),
+                raws[c][:, :, on_vector:].rearrange("p j (c i) -> p c j i", i=4),
+            )
+            nc.vector.tensor_copy(
+                grouped[:, :on_vector, :].rearrange("p (c i) j -> p c j i", i=4),
+                raws[c][:, :, :on_vector].rearrange("p j (c i) -> p c j i", i=4),
+            )
+            nc.vector.quantize_mx(
+                x_codes[:, t0 : t0 + width].bitcast(FP8X4),
+                x_scales[:, t0 : t0 + width],
+                grouped[:].rearrange("p t j -> p (t j)"),
+            )
+            t0 += width
+
+        slot_codes, slot_scales = {}, {}
+        a_ps, b_ps, sig, h_words, turned, h_grouped, h_codes, h_scales, y_ps = {}, {}, {}, {}, {}, {}, {}, {}, {}
+
+        def slot_offsets(e):
+            return offs_sb[:, e * C // PER_COL : (e + 1) * C // PER_COL]
+
+        def gather_codes(e):
+            slot_codes[e] = keep.tile([P, C], U32, name=f"slot_codes{e}", align_bytes=64)
+            nc.vector.tensor_copy(slot_codes[e][:], x_codes[:].indirect(slot_offsets(e)))
+
+        def gather_scales(e):
+            slot_scales[e] = keep.tile([P, C], U8, name=f"slot_scales{e}", align_bytes=64)
+            nc.vector.tensor_copy(slot_scales[e][:], x_scales[:].indirect(slot_offsets(e)))
+
+        def first_layer(blk):
+            e, half = divmod(blk, 2)
+            cols = slice(half * P, (half + 1) * P)
+            a_ps[blk] = psum.tile([P, H], F32, name="a_ps", tag="a_ps", bufs=2)
+            b_ps[blk] = psum.tile([P, H], F32, name="b_ps", tag="b_ps", bufs=3)
+            for acc, words, plane in ((a_ps[blk], w1_sb, w1_plane), (b_ps[blk], w3_sb, w3_plane)):
+                nc.tensor.matmul_mx(
+                    acc[:],
+                    lhsT=slot_codes[e][:, cols].bitcast(FP8X4),
+                    lhsT_scale=slot_scales[e][:, cols],
+                    rhs=words[:, e, :].bitcast(FP4X4),
+                    rhs_scale=plane[:, e, :],
+                    start=True,
+                    stop=True,
+                )
+
+        def sigmoid(blk):
+            sig[blk] = ring.tile([P, H], F32, name="sig")
+            nc.scalar.activation(
+                sig[blk][:].rearrange("s (u p v) -> s u p v", u=2, v=2),
+                a_ps[blk][:].rearrange("s (p u v) -> s u p v", u=2, v=2),
+                SIGMOID,
+            )
+
+        def gated(blk):
+            h = ring.tile([P, H], BF16, name="h", bufs=4)
+            nc.vector.tensor_tensor(
+                h[:].rearrange("s (u p v) -> s u p v", u=2, v=2),
+                b_ps[blk][:].rearrange("s (p u v) -> s u p v", u=2, v=2),
+                sig[blk][:].rearrange("s (u p v) -> s u p v", u=2, v=2),
+                MULT,
+            )
+            h_words[blk] = h[:].bitcast(F32)
+
+        def turn(run):
+            turned[run] = psum.tile([P, len(run), 2, P], F32, name="turned", tag="turned", bufs=2)
+            for b, blk in enumerate(run):
+                for u in range(2):
+                    nc.tensor.transpose(turned[run][:, b, u, :], h_words[blk][:, u * P : (u + 1) * P], ident[:])
+
+        def copy_turned(run, copy):
+            h_grouped[run] = ring.tile([P, 4 * P * len(run)], BF16, name="h_grouped", align_bytes=64)
+            copy(
+                h_grouped[run][:].bitcast(F32).rearrange("p (b s u) -> p b s u", b=len(run), u=2),
+                turned[run][:].rearrange("p b u s -> p b s u"),
+            )
+
+        def quantise_h(run):
+            h_codes[run] = ring.tile([P, P * len(run)], U32, name="h_codes", align_bytes=64)
+            h_scales[run] = ring.tile([P, P * len(run)], U8, name="h_scales", align_bytes=64)
+            nc.vector.quantize_mx(h_codes[run][:].bitcast(FP8X4), h_scales[run][:], h_grouped[run][:])
+
+        def second_layer(run, tag="y_ps", bufs=1):
+            e = run[0] // 2
+            y_ps[run] = psum.tile([P, P * len(run)], F32, name="y_ps", tag=tag, bufs=bufs)
+            nc.tensor.matmul_mx(
+                y_ps[run][:],
+                lhsT=w2_sb[:, e, :].bitcast(FP4X4),
+                lhsT_scale=w2_plane[:, e, :],
+                rhs=h_codes[run][:].bitcast(FP8X4),
+                rhs_scale=h_scales[run][:],
+                start=True,
+                stop=True,
+            )
+
+        def copy_y(run, copy):
+            copy(y_all[:, run[0] * P : (run[-1] + 1) * P], y_ps[run][:])
+
+        for e in range(AHEAD):
+            gather_codes(e)
+            gather_scales(e)
+        for blk in range(3):
+            first_layer(blk)
+            if blk == 0:
+                sigmoid(0)
+        for e in range(E):
+            first, second = 2 * e, 2 * e + 1
+            gathering = e + AHEAD < E
+            before = (first - 2, first - 1)
+            earlier = (first - 4, first - 3)
+            gated(first)
+            if e >= 1:
+                turn(before)
+            if e >= 2:
+                second_layer(earlier)
+            sigmoid(second)
+            if gathering:
+                gather_codes(e + AHEAD)
+            elif e >= 2:
+                copy_y(earlier, nc.vector.tensor_copy)
+            if e >= 1:
+                copy_turned(before, nc.scalar.copy)
+            if e + 1 < E:
+                first_layer(second + 2)
+            else:
+                turn((first,))
+            gated(second)
+            if e + 1 < E:
+                sigmoid(first + 2)
+            else:
+                copy_turned((first,), nc.scalar.copy)
+            if gathering:
+                gather_scales(e + AHEAD)
+            if e + 2 < E:
+                first_layer(first + 4)
+            if e >= 1:
+                quantise_h(before)
+            if gathering and e >= 2:
+                copy_y(earlier, nc.scalar.copy)
+        before, first, second = (2 * E - 4, 2 * E - 3), (2 * E - 2,), (2 * E - 1,)
+        turn(second)
+        second_layer(before)
+        quantise_h(first)
+        copy_y(before, nc.scalar.copy)
+        copy_turned(second, nc.vector.tensor_copy)
+        second_layer(first, "a_ps", 2)
+        quantise_h(second)
+        copy_y(first, nc.scalar.copy)
+        second_layer(second, "a_ps", 2)
+        copy_y(second, nc.vector.tensor_copy)
+
+        def weighted(r, t0, width):
+            term = ring.tile([P, width], F32, name=f"term{r}", tag=f"term{r}", bufs=2)
+            cols = pos_sb[r][:, t0 // PER_COL : (t0 + width) // PER_COL]
+            nc.vector.tensor_tensor(term[:], y_all[:].indirect(cols), gate_sb[r][:, t0 : t0 + width], MULT)
+            return term
+
+        t0 = 0
+        for width in PE_CHUNKS:
+            terms = [weighted(r, t0, width) for r in range(TOP)]
+            summed = psum.tile([P, width], F32, name="summed", tag="a_ps", bufs=2)
+            for b0 in range(0, width, P):
+                for r in range(TOP):
+                    nc.tensor.matmul(
+                        summed[:, b0 : b0 + P],
+                        lhsT=terms[r][:, b0 : b0 + P],
+                        rhs=ident[:],
+                        start=(r == 0),
+                        stop=(r == TOP - 1),
+                        is_transpose=True,
+                    )
+            summed_sb = ring.tile([P, width], F32, name="summed_sb", bufs=2)
+            nc.scalar.copy(summed_sb[:], summed[:])
+            back = psum.tile([P, width], F32, name="back", tag="b_ps", bufs=3)
+            for b0 in range(0, width, P):
+                nc.tensor.transpose(back[:, b0 : b0 + P], summed_sb[:, b0 : b0 + P], ident[:])
+            result = ring.tile([P, width], F32, name="result")
+            nc.scalar.copy(result[:], back[:])
+            nc.sync.dma_start(out[:, t0 : t0 + width], result[:])
+            t0 += width
+
+        terms = [weighted(r, t0, LAST_CHUNK) for r in range(3)]
+        sum01 = keep.tile([P, LAST_CHUNK], F32, name="sum01")
+        nc.vector.tensor_tensor(sum01[:], terms[0][:], terms[1][:], ADD)
+        terms.append(weighted(3, t0, LAST_CHUNK))
+        sum012 = keep.tile([P, LAST_CHUNK], F32, name="sum012")
+        nc.vector.tensor_tensor(sum012[:], sum01[:], terms[2][:], ADD)
+        last = keep.tile([P, LAST_CHUNK], F32, name="last")
+        nc.vector.tensor_tensor(last[:], sum012[:], terms[3][:], ADD)
+        nc.sync.dma_start(out[:, t0:], last[:])

@@ -25,7 +25,7 @@ P = 128
 PER_COL = 16
 X_CHUNKS = ((512, 256), (512, 256), (256, 160), (256, 160))
 AHEAD = 3
-PE_CHUNKS = (512, 512, 256)
+CHUNK = 256
 LAST_CHUNK = 256
 
 
@@ -59,7 +59,6 @@ def tile_moe_ecr_glu_sigmoid_kernel(
         nc.vector.memset(y_all[:, S:], 0.0)
 
         offs_sb = lists.tile([P, S // PER_COL], U16, name="offs_sb")
-        nc.sync.dma_start(offs_sb[:], offs)
 
         x_rows = xT.rearrange("(p j) t -> p j t", j=4)
         raws = []
@@ -86,18 +85,17 @@ def tile_moe_ecr_glu_sigmoid_kernel(
                     dst[32 * quad : 32 * quad + 4, e0:e1, :].bitcast(I32), rows[4 * quad : 4 * quad + 4].bitcast(I32)
                 )
 
+        nc.sync.dma_start(offs_sb[:], offs)
+        load_scales(w1_plane, w1_scales, 0, E)
+        load_scales(w3_plane, w3_scales, 0, E)
         load_words(w1_sb, w1_words, 0, 2)
         load_words(w3_sb, w3_words, 0, 2)
-        load_scales(w1_plane, w1_scales, 0, 4)
-        load_scales(w3_plane, w3_scales, 0, 4)
         load_scales(w2_plane, w2_scales, 0, E)
         load_words(w2_sb, w2_words, 0, E)
-        load_words(w1_sb, w1_words, 2, 4)
-        load_words(w3_sb, w3_words, 2, 4)
-        load_scales(w1_plane, w1_scales, 4, E)
-        load_scales(w3_plane, w3_scales, 4, E)
-        load_words(w1_sb, w1_words, 4, E)
-        load_words(w3_sb, w3_words, 4, E)
+        load_words(w1_sb, w1_words, 2, 5)
+        load_words(w3_sb, w3_words, 2, 5)
+        load_words(w1_sb, w1_words, 5, E)
+        load_words(w3_sb, w3_words, 5, E)
         pos_sb = []
         for r, pos in enumerate((pos1, pos2, pos3, pos4)):
             tile = lists.tile([P, T // PER_COL], U16, name=f"pos_sb{r}")
@@ -134,11 +132,11 @@ def tile_moe_ecr_glu_sigmoid_kernel(
             return offs_sb[:, e * C // PER_COL : (e + 1) * C // PER_COL]
 
         def gather_codes(e):
-            slot_codes[e] = keep.tile([P, C], U32, name=f"slot_codes{e}", align_bytes=64)
+            slot_codes[e] = ring.tile([P, C], U32, name="slot_codes", align_bytes=64, bufs=AHEAD)
             nc.vector.tensor_copy(slot_codes[e][:], x_codes[:].indirect(slot_offsets(e)))
 
         def gather_scales(e):
-            slot_scales[e] = keep.tile([P, C], U8, name=f"slot_scales{e}", align_bytes=64)
+            slot_scales[e] = ring.tile([P, C], U8, name="slot_scales", align_bytes=64, bufs=AHEAD)
             nc.vector.tensor_copy(slot_scales[e][:], x_scales[:].indirect(slot_offsets(e)))
 
         def first_layer(blk):
@@ -263,34 +261,48 @@ def tile_moe_ecr_glu_sigmoid_kernel(
         copy_y(second, nc.vector.tensor_copy)
 
         def weighted(r, t0, width):
-            term = ring.tile([P, width], F32, name=f"term{r}", tag=f"term{r}", bufs=2)
+            term = ring.tile([P, width], F32, name=f"term{r}", tag=f"term{r}", bufs=3)
             cols = pos_sb[r][:, t0 // PER_COL : (t0 + width) // PER_COL]
             nc.vector.tensor_tensor(term[:], y_all[:].indirect(cols), gate_sb[r][:, t0 : t0 + width], MULT)
             return term
 
-        t0 = 0
-        for width in PE_CHUNKS:
-            terms = [weighted(r, t0, width) for r in range(TOP)]
-            summed = psum.tile([P, width], F32, name="summed", tag="a_ps", bufs=2)
-            for b0 in range(0, width, P):
-                for r in range(TOP):
+        summed = {}
+
+        def add_terms(chunk):
+            t0 = chunk * CHUNK
+            summed[chunk] = [
+                psum.tile([P, P], F32, name="summed", tag=tag, bufs=2) for tag in ("a_ps", "turned")
+            ]
+            for r in range(TOP):
+                term = weighted(r, t0, CHUNK)
+                for b in range(2):
                     nc.tensor.matmul(
-                        summed[:, b0 : b0 + P],
-                        lhsT=terms[r][:, b0 : b0 + P],
+                        summed[chunk][b][:],
+                        lhsT=term[:, b * P : (b + 1) * P],
                         rhs=ident[:],
                         start=(r == 0),
                         stop=(r == TOP - 1),
                         is_transpose=True,
                     )
-            summed_sb = ring.tile([P, width], F32, name="summed_sb", bufs=2)
-            nc.scalar.copy(summed_sb[:], summed[:])
-            back = psum.tile([P, width], F32, name="back", tag="b_ps", bufs=3)
-            for b0 in range(0, width, P):
-                nc.tensor.transpose(back[:, b0 : b0 + P], summed_sb[:, b0 : b0 + P], ident[:])
-            result = ring.tile([P, width], F32, name="result")
+                if r == 1 and chunk >= 1:
+                    turn_back(chunk - 1)
+            summed_sb[chunk] = ring.tile([P, CHUNK], F32, name="summed_sb", bufs=2)
+            for b in range(2):
+                nc.scalar.copy(summed_sb[chunk][:, b * P : (b + 1) * P], summed[chunk][b][:])
+
+        def turn_back(chunk):
+            back = psum.tile([P, CHUNK], F32, name="back", tag="b_ps", bufs=3)
+            for b in range(2):
+                nc.tensor.transpose(back[:, b * P : (b + 1) * P], summed_sb[chunk][:, b * P : (b + 1) * P], ident[:])
+            result = ring.tile([P, CHUNK], F32, name="result")
             nc.scalar.copy(result[:], back[:])
-            nc.sync.dma_start(out[:, t0 : t0 + width], result[:])
-            t0 += width
+            nc.sync.dma_start(out[:, chunk * CHUNK : (chunk + 1) * CHUNK], result[:])
+
+        summed_sb = {}
+        for chunk in range(T // CHUNK - 1):
+            add_terms(chunk)
+        turn_back(T // CHUNK - 2)
+        t0 = T - LAST_CHUNK
 
         terms = [weighted(r, t0, LAST_CHUNK) for r in range(3)]
         sum01 = keep.tile([P, LAST_CHUNK], F32, name="sum01")

@@ -22,11 +22,18 @@ ADD = mybir.AluOpType.add
 SIGMOID = mybir.ActivationFunctionType.Sigmoid
 
 P = 128
+PACK = 4
 PER_COL = 16
-X_CHUNKS = ((512, 256), (512, 256), (256, 160), (256, 160))
-AHEAD = 3
-CHUNK = 256
-LAST_CHUNK = 256
+BLOCKS = S // P
+
+X_PIECES = ((512, 256), (512, 256), (256, 128), (128, 64), (128, 80))
+W1_LOADS = ((0, 2), (2, 5), (5, E))
+W3_LOADS = ((0, 4), (4, E))
+GATE_PIECE = 512
+SUM_BANKS, TURN_BANKS, Y_BANKS = 5, 2, 1
+EARLY_W3 = 3
+TENSOR_PIECES = (256, 256, 256, 256, 256)
+VECTOR_PIECE = 256
 
 
 def tile_moe_ecr_glu_sigmoid_kernel(
@@ -38,11 +45,6 @@ def tile_moe_ecr_glu_sigmoid_kernel(
         keep = ctx.enter_context(tc.tile_pool(name="keep", bufs=1))
         ring = ctx.enter_context(tc.tile_pool(name="ring", bufs=3))
         psum = ctx.enter_context(tc.psum_pool(name="psum", bufs=2))
-
-        warm = keep.tile([P, 8], F32, name="warm")
-        warm_out = keep.tile([P, 8], F32, name="warm_out")
-        nc.vector.memset(warm[:], 0.0)
-        nc.scalar.activation(warm_out[:], warm[:], SIGMOID)
 
         x_codes = keep.tile([P, T], U32, name="x_codes", align_bytes=64)
         x_scales = keep.tile([P, T], U8, name="x_scales", align_bytes=64)
@@ -58,16 +60,16 @@ def tile_moe_ecr_glu_sigmoid_kernel(
         y_all = keep.tile([P, S + PAD], F32, name="y_all")
         nc.vector.memset(y_all[:, S:], 0.0)
 
-        offs_sb = lists.tile([P, S // PER_COL], U16, name="offs_sb")
-
-        x_rows = xT.rearrange("(p j) t -> p j t", j=4)
-        raws = []
+        x_rows = xT.rearrange("(p j) t -> p j t", j=PACK)
+        x_raw = []
         t0 = 0
-        for c, (width, on_vector) in enumerate(X_CHUNKS):
-            raw = keep.tile([P, 4, width], F32, name=f"x_raw{c}")
+        for piece, (width, on_vector) in enumerate(X_PIECES):
+            raw = keep.tile([P, PACK, width], F32, name=f"x_raw{piece}")
             nc.sync.dma_start(raw[:], x_rows[:, :, t0 : t0 + width])
-            raws.append(raw)
+            x_raw.append(raw)
             t0 += width
+        offs_sb = lists.tile([P, S // PER_COL], U16, name="offs_sb")
+        nc.sync.dma_start(offs_sb[:], offs)
 
         w1_sb = keep.tile([P, E, 2 * H], U8, name="w1_sb", align_bytes=64)
         w3_sb = keep.tile([P, E, 2 * H], U8, name="w3_sb", align_bytes=64)
@@ -78,45 +80,41 @@ def tile_moe_ecr_glu_sigmoid_kernel(
                 dst[:, e0:e1, :].bitcast(I32), src[e0:e1].rearrange("e s p c -> p (e s) c").bitcast(I32)
             )
 
-        def load_scales(dst, src, e0, e1):
-            rows = src[e0:e1].rearrange("e s q c -> q (e s) c")
-            for quad in range(4):
+        def load_scales(dst, src):
+            rows = src.rearrange("e s q c -> q (e s) c")
+            for quad in (0, 2, 1, 3):
                 nc.sync.dma_start(
-                    dst[32 * quad : 32 * quad + 4, e0:e1, :].bitcast(I32), rows[4 * quad : 4 * quad + 4].bitcast(I32)
+                    dst[32 * quad : 32 * quad + 4, :, :].bitcast(I32), rows[4 * quad : 4 * quad + 4].bitcast(I32)
                 )
 
-        nc.sync.dma_start(offs_sb[:], offs)
-        load_scales(w1_plane, w1_scales, 0, E)
-        load_scales(w3_plane, w3_scales, 0, E)
-        load_words(w1_sb, w1_words, 0, 2)
-        load_words(w3_sb, w3_words, 0, 2)
-        load_scales(w2_plane, w2_scales, 0, E)
+        load_scales(w1_plane, w1_scales)
+        for e0, e1 in W1_LOADS:
+            load_words(w1_sb, w1_words, e0, e1)
+        load_scales(w3_plane, w3_scales)
+        for e0, e1 in W3_LOADS:
+            load_words(w3_sb, w3_words, e0, e1)
+        load_scales(w2_plane, w2_scales)
         load_words(w2_sb, w2_words, 0, E)
-        load_words(w1_sb, w1_words, 2, 5)
-        load_words(w3_sb, w3_words, 2, 5)
-        load_words(w1_sb, w1_words, 5, E)
-        load_words(w3_sb, w3_words, 5, E)
         pos_sb = []
         for r, pos in enumerate((pos1, pos2, pos3, pos4)):
-            tile = lists.tile([P, T // PER_COL], U16, name=f"pos_sb{r}")
-            nc.sync.dma_start(tile[:], pos)
-            pos_sb.append(tile)
-        gate_sb = []
-        for r in range(TOP):
-            tile = keep.tile([P, T], F32, name=f"gate_sb{r}")
-            nc.sync.dma_start(tile[:], gate[r])
-            gate_sb.append(tile)
+            pos_tile = lists.tile([P, T // PER_COL], U16, name=f"pos_sb{r}")
+            nc.sync.dma_start(pos_tile[:], pos)
+            pos_sb.append(pos_tile)
+        gate_sb = keep.tile([P, TOP, T], F32, name="gate_sb")
+        gate_rows = gate.rearrange("r p t -> p r t")
+        for t0 in range(0, T, GATE_PIECE):
+            nc.sync.dma_start(gate_sb[:, :, t0 : t0 + GATE_PIECE], gate_rows[:, :, t0 : t0 + GATE_PIECE])
 
         t0 = 0
-        for c, (width, on_vector) in enumerate(X_CHUNKS):
-            grouped = keep.tile([P, width, 4], BF16, name=f"x_grouped{c}", align_bytes=64)
+        for piece, (width, on_vector) in enumerate(X_PIECES):
+            grouped = keep.tile([P, width, PACK], BF16, name=f"x_grouped{piece}", align_bytes=64)
             nc.scalar.copy(
                 grouped[:, on_vector:, :].rearrange("p (c i) j -> p c j i", i=4),
-                raws[c][:, :, on_vector:].rearrange("p j (c i) -> p c j i", i=4),
+                x_raw[piece][:, :, on_vector:].rearrange("p j (c i) -> p c j i", i=4),
             )
             nc.vector.tensor_copy(
                 grouped[:, :on_vector, :].rearrange("p (c i) j -> p c j i", i=4),
-                raws[c][:, :, :on_vector].rearrange("p j (c i) -> p c j i", i=4),
+                x_raw[piece][:, :, :on_vector].rearrange("p j (c i) -> p c j i", i=4),
             )
             nc.vector.quantize_mx(
                 x_codes[:, t0 : t0 + width].bitcast(FP8X4),
@@ -126,72 +124,67 @@ def tile_moe_ecr_glu_sigmoid_kernel(
             t0 += width
 
         slot_codes, slot_scales = {}, {}
-        a_ps, b_ps, sig, h_words, turned, h_grouped, h_codes, h_scales, y_ps = {}, {}, {}, {}, {}, {}, {}, {}, {}
+        b_ps, sig, h_pairs = {}, {}, {}
+        h_grouped, h_codes, h_scales, y_ps = {}, {}, {}, {}
 
-        def slot_offsets(e):
-            return offs_sb[:, e * C // PER_COL : (e + 1) * C // PER_COL]
+        def gather_tokens(e):
+            offsets = offs_sb[:, e * C // PER_COL : (e + 1) * C // PER_COL]
+            slot_codes[e] = keep.tile([P, C], U32, name=f"slot_codes{e}", align_bytes=64)
+            nc.vector.tensor_copy(slot_codes[e][:], x_codes[:].indirect(offsets))
+            slot_scales[e] = keep.tile([P, C], U8, name=f"slot_scales{e}", align_bytes=64)
+            nc.vector.tensor_copy(slot_scales[e][:], x_scales[:].indirect(offsets))
 
-        def gather_codes(e):
-            slot_codes[e] = ring.tile([P, C], U32, name="slot_codes", align_bytes=64, bufs=AHEAD)
-            nc.vector.tensor_copy(slot_codes[e][:], x_codes[:].indirect(slot_offsets(e)))
-
-        def gather_scales(e):
-            slot_scales[e] = ring.tile([P, C], U8, name="slot_scales", align_bytes=64, bufs=AHEAD)
-            nc.vector.tensor_copy(slot_scales[e][:], x_scales[:].indirect(slot_offsets(e)))
-
-        def first_layer(blk):
+        def first_layer(blk, words, plane):
             e, half = divmod(blk, 2)
             cols = slice(half * P, (half + 1) * P)
-            a_ps[blk] = psum.tile([P, H], F32, name="a_ps", tag="a_ps", bufs=2)
-            b_ps[blk] = psum.tile([P, H], F32, name="b_ps", tag="b_ps", bufs=3)
-            for acc, words, plane in ((a_ps[blk], w1_sb, w1_plane), (b_ps[blk], w3_sb, w3_plane)):
-                nc.tensor.matmul_mx(
-                    acc[:],
-                    lhsT=slot_codes[e][:, cols].bitcast(FP8X4),
-                    lhsT_scale=slot_scales[e][:, cols],
-                    rhs=words[:, e, :].bitcast(FP4X4),
-                    rhs_scale=plane[:, e, :],
-                    start=True,
-                    stop=True,
-                )
-
-        def sigmoid(blk):
-            sig[blk] = ring.tile([P, H], F32, name="sig")
-            nc.scalar.activation(
-                sig[blk][:].rearrange("s (u p v) -> s u p v", u=2, v=2),
-                a_ps[blk][:].rearrange("s (p u v) -> s u p v", u=2, v=2),
-                SIGMOID,
+            acc = psum.tile([P, H], F32, name="acc", tag="sums", bufs=SUM_BANKS)
+            nc.tensor.matmul_mx(
+                acc[:],
+                lhsT=slot_codes[e][:, cols].bitcast(FP8X4),
+                lhsT_scale=slot_scales[e][:, cols],
+                rhs=words[:, e, :].bitcast(FP4X4),
+                rhs_scale=plane[:, e, :],
+                start=True,
+                stop=True,
             )
+            return acc
+
+        def as_stored(tile):
+            return tile[:].rearrange("s (u p v) -> s u p v", u=2, v=2)
+
+        def as_summed(tile):
+            return tile[:].rearrange("s (p u v) -> s u p v", u=2, v=2)
+
+        def sigmoid_of_w1(blk):
+            a_ps = first_layer(blk, w1_sb, w1_plane)
+            sig[blk] = keep.tile([P, H], F32, name=f"sig{blk}")
+            nc.scalar.activation(as_stored(sig[blk]), as_summed(a_ps), SIGMOID)
+
+        def product_w3(blk):
+            b_ps[blk] = first_layer(blk, w3_sb, w3_plane)
 
         def gated(blk):
             h = ring.tile([P, H], BF16, name="h", bufs=4)
-            nc.vector.tensor_tensor(
-                h[:].rearrange("s (u p v) -> s u p v", u=2, v=2),
-                b_ps[blk][:].rearrange("s (p u v) -> s u p v", u=2, v=2),
-                sig[blk][:].rearrange("s (u p v) -> s u p v", u=2, v=2),
-                MULT,
-            )
-            h_words[blk] = h[:].bitcast(F32)
+            nc.vector.tensor_tensor(as_stored(h), as_summed(b_ps[blk]), as_stored(sig[blk]), MULT)
+            h_pairs[blk] = h[:].bitcast(F32)
 
         def turn(run):
-            turned[run] = psum.tile([P, len(run), 2, P], F32, name="turned", tag="turned", bufs=2)
+            turned = psum.tile([P, len(run), 2, P], F32, name="turned", tag="turned", bufs=TURN_BANKS)
             for b, blk in enumerate(run):
                 for u in range(2):
-                    nc.tensor.transpose(turned[run][:, b, u, :], h_words[blk][:, u * P : (u + 1) * P], ident[:])
-
-        def copy_turned(run, copy):
-            h_grouped[run] = ring.tile([P, 4 * P * len(run)], BF16, name="h_grouped", align_bytes=64)
-            copy(
+                    nc.tensor.transpose(turned[:, b, u, :], h_pairs[blk][:, u * P : (u + 1) * P], ident[:])
+            h_grouped[run] = ring.tile([P, PACK * P * len(run)], BF16, name="h_grouped", align_bytes=64, bufs=4)
+            nc.scalar.copy(
                 h_grouped[run][:].bitcast(F32).rearrange("p (b s u) -> p b s u", b=len(run), u=2),
-                turned[run][:].rearrange("p b u s -> p b s u"),
+                turned[:].rearrange("p b u s -> p b s u"),
             )
 
         def quantise_h(run):
-            h_codes[run] = ring.tile([P, P * len(run)], U32, name="h_codes", align_bytes=64)
-            h_scales[run] = ring.tile([P, P * len(run)], U8, name="h_scales", align_bytes=64)
+            h_codes[run] = ring.tile([P, P * len(run)], U32, name="h_codes", align_bytes=64, bufs=4)
+            h_scales[run] = ring.tile([P, P * len(run)], U8, name="h_scales", align_bytes=64, bufs=4)
             nc.vector.quantize_mx(h_codes[run][:].bitcast(FP8X4), h_scales[run][:], h_grouped[run][:])
 
-        def second_layer(run, tag="y_ps", bufs=1):
+        def second_layer(run, tag, bufs):
             e = run[0] // 2
             y_ps[run] = psum.tile([P, P * len(run)], F32, name="y_ps", tag=tag, bufs=bufs)
             nc.tensor.matmul_mx(
@@ -207,109 +200,92 @@ def tile_moe_ecr_glu_sigmoid_kernel(
         def copy_y(run, copy):
             copy(y_all[:, run[0] * P : (run[-1] + 1) * P], y_ps[run][:])
 
-        for e in range(AHEAD):
-            gather_codes(e)
-            gather_scales(e)
-        for blk in range(3):
-            first_layer(blk)
-            if blk == 0:
-                sigmoid(0)
+        def both_blocks(e):
+            return (2 * e, 2 * e + 1)
+
         for e in range(E):
-            first, second = 2 * e, 2 * e + 1
-            gathering = e + AHEAD < E
-            before = (first - 2, first - 1)
-            earlier = (first - 4, first - 3)
-            gated(first)
-            if e >= 1:
-                turn(before)
-            if e >= 2:
-                second_layer(earlier)
-            sigmoid(second)
-            if gathering:
-                gather_codes(e + AHEAD)
-            elif e >= 2:
-                copy_y(earlier, nc.vector.tensor_copy)
-            if e >= 1:
-                copy_turned(before, nc.scalar.copy)
-            if e + 1 < E:
-                first_layer(second + 2)
-            else:
-                turn((first,))
-            gated(second)
-            if e + 1 < E:
-                sigmoid(first + 2)
-            else:
-                copy_turned((first,), nc.scalar.copy)
-            if gathering:
-                gather_scales(e + AHEAD)
-            if e + 2 < E:
-                first_layer(first + 4)
-            if e >= 1:
-                quantise_h(before)
-            if gathering and e >= 2:
-                copy_y(earlier, nc.scalar.copy)
-        before, first, second = (2 * E - 4, 2 * E - 3), (2 * E - 2,), (2 * E - 1,)
-        turn(second)
-        second_layer(before)
-        quantise_h(first)
-        copy_y(before, nc.scalar.copy)
-        copy_turned(second, nc.vector.tensor_copy)
-        second_layer(first, "a_ps", 2)
-        quantise_h(second)
-        copy_y(first, nc.scalar.copy)
-        second_layer(second, "a_ps", 2)
-        copy_y(second, nc.vector.tensor_copy)
+            gather_tokens(e)
+            if e == E - 1:
+                for blk in range(EARLY_W3):
+                    product_w3(blk)
+            for blk in both_blocks(e):
+                sigmoid_of_w1(blk)
+
+        next_w3 = EARLY_W3
+        for blk in range(BLOCKS):
+            e, half = divmod(blk, 2)
+            gated(blk)
+            if half == 0 and 2 <= e < E - 1:
+                quantise_h(both_blocks(e - 2))
+            if half == 1 and e < E - 1:
+                turn(both_blocks(e))
+            if half == 1 and 2 <= e < E - 1:
+                second_layer(both_blocks(e - 2), "y", Y_BANKS)
+                copy_y(both_blocks(e - 2), nc.scalar.copy)
+            if blk == BLOCKS - 2:
+                turn((blk,))
+            ahead = EARLY_W3 if blk < EARLY_W3 - 1 else SUM_BANKS
+            while next_w3 <= min(blk + ahead, BLOCKS - 1):
+                product_w3(next_w3)
+                next_w3 += 1
+
+        last_runs = (both_blocks(E - 3), both_blocks(E - 2), (BLOCKS - 2,), (BLOCKS - 1,))
+        turn(last_runs[-1])
+        for run in last_runs:
+            quantise_h(run)
+            second_layer(run, "sums", SUM_BANKS)
+        for run in last_runs[:-1]:
+            copy_y(run, nc.scalar.copy)
+        copy_y(last_runs[-1], nc.vector.tensor_copy)
 
         def weighted(r, t0, width):
-            term = ring.tile([P, width], F32, name=f"term{r}", tag=f"term{r}", bufs=3)
-            cols = pos_sb[r][:, t0 // PER_COL : (t0 + width) // PER_COL]
-            nc.vector.tensor_tensor(term[:], y_all[:].indirect(cols), gate_sb[r][:, t0 : t0 + width], MULT)
+            term = ring.tile([P, width], F32, name=f"term{r}")
+            offsets = pos_sb[r][:, t0 // PER_COL : (t0 + width) // PER_COL]
+            nc.vector.tensor_tensor(term[:], y_all[:].indirect(offsets), gate_sb[:, r, t0 : t0 + width], MULT)
             return term
 
-        summed = {}
+        summed_sb = {}
 
-        def add_terms(chunk):
-            t0 = chunk * CHUNK
-            summed[chunk] = [
-                psum.tile([P, P], F32, name="summed", tag=tag, bufs=2) for tag in ("a_ps", "turned")
-            ]
+        def add_terms(piece):
+            t0, width = sum(TENSOR_PIECES[:piece]), TENSOR_PIECES[piece]
+            summed = [psum.tile([P, P], F32, name="summed", tag="sums", bufs=SUM_BANKS) for b in range(width // P)]
             for r in range(TOP):
-                term = weighted(r, t0, CHUNK)
-                for b in range(2):
+                term = weighted(r, t0, width)
+                for b in range(width // P):
                     nc.tensor.matmul(
-                        summed[chunk][b][:],
+                        summed[b][:],
                         lhsT=term[:, b * P : (b + 1) * P],
                         rhs=ident[:],
                         start=(r == 0),
                         stop=(r == TOP - 1),
                         is_transpose=True,
                     )
-                if r == 1 and chunk >= 1:
-                    turn_back(chunk - 1)
-            summed_sb[chunk] = ring.tile([P, CHUNK], F32, name="summed_sb", bufs=2)
-            for b in range(2):
-                nc.scalar.copy(summed_sb[chunk][:, b * P : (b + 1) * P], summed[chunk][b][:])
+                if r == TOP // 2 - 1 and piece >= 1:
+                    turn_back(piece - 1)
+            summed_sb[piece] = ring.tile([P, width], F32, name="summed_sb", bufs=2)
+            for b in range(width // P):
+                nc.scalar.copy(summed_sb[piece][:, b * P : (b + 1) * P], summed[b][:])
 
-        def turn_back(chunk):
-            back = psum.tile([P, CHUNK], F32, name="back", tag="b_ps", bufs=3)
-            for b in range(2):
-                nc.tensor.transpose(back[:, b * P : (b + 1) * P], summed_sb[chunk][:, b * P : (b + 1) * P], ident[:])
-            result = ring.tile([P, CHUNK], F32, name="result")
+        def turn_back(piece):
+            t0, width = sum(TENSOR_PIECES[:piece]), TENSOR_PIECES[piece]
+            back = psum.tile([P, width], F32, name="back", tag="turned", bufs=TURN_BANKS)
+            for b in range(width // P):
+                nc.tensor.transpose(back[:, b * P : (b + 1) * P], summed_sb[piece][:, b * P : (b + 1) * P], ident[:])
+            result = ring.tile([P, width], F32, name="result")
             nc.scalar.copy(result[:], back[:])
-            nc.sync.dma_start(out[:, chunk * CHUNK : (chunk + 1) * CHUNK], result[:])
+            nc.scalar.dma_start(out[:, t0 : t0 + width], result[:])
 
-        summed_sb = {}
-        for chunk in range(T // CHUNK - 1):
-            add_terms(chunk)
-        turn_back(T // CHUNK - 2)
-        t0 = T - LAST_CHUNK
+        for piece in range(len(TENSOR_PIECES)):
+            add_terms(piece)
+        turn_back(len(TENSOR_PIECES) - 1)
 
-        terms = [weighted(r, t0, LAST_CHUNK) for r in range(3)]
-        sum01 = keep.tile([P, LAST_CHUNK], F32, name="sum01")
-        nc.vector.tensor_tensor(sum01[:], terms[0][:], terms[1][:], ADD)
-        terms.append(weighted(3, t0, LAST_CHUNK))
-        sum012 = keep.tile([P, LAST_CHUNK], F32, name="sum012")
-        nc.vector.tensor_tensor(sum012[:], sum01[:], terms[2][:], ADD)
-        last = keep.tile([P, LAST_CHUNK], F32, name="last")
-        nc.vector.tensor_tensor(last[:], sum012[:], terms[3][:], ADD)
-        nc.sync.dma_start(out[:, t0:], last[:])
+        t0 = T - VECTOR_PIECE
+        terms = [weighted(r, t0, VECTOR_PIECE) for r in range(TOP - 1)]
+        two_terms = keep.tile([P, VECTOR_PIECE], F32, name="two_terms")
+        nc.vector.tensor_tensor(two_terms[:], terms[0][:], terms[1][:], ADD)
+        terms.append(weighted(TOP - 1, t0, VECTOR_PIECE))
+        three_terms = keep.tile([P, VECTOR_PIECE], F32, name="three_terms")
+        nc.vector.tensor_tensor(three_terms[:], two_terms[:], terms[2][:], ADD)
+        four_terms = keep.tile([P, VECTOR_PIECE], F32, name="four_terms")
+        nc.vector.tensor_tensor(four_terms[:], three_terms[:], terms[3][:], ADD)
+        nc.sync.dma_start(out[:, t0:], four_terms[:])

from contextlib import ExitStack

import concourse.mybir as mybir
from concourse.masks import make_identity

K, T, E, C, H, N = 512, 1536, 8, 256, 512, 128
TOP = 4
PAD = 64
S = E * C
FLOPS = 2 * S * (2 * K * H + H * N)

F32 = mybir.dt.float32
BF16 = mybir.dt.bfloat16
I32 = mybir.dt.int32
U32 = mybir.dt.uint32
U16 = mybir.dt.uint16
U8 = mybir.dt.uint8
FP8X4 = mybir.dt.float8_e4m3fn_x4
FP4X4 = mybir.dt.float4_e2m1fn_x4
MULT = mybir.AluOpType.mult
ADD = mybir.AluOpType.add
SIGMOID = mybir.ActivationFunctionType.Sigmoid

P = 128
PACK = 4
PER_COL = 16
BLOCKS = S // P

X_PIECES = ((512, 256), (512, 256), (256, 128), (128, 64), (128, 80))
W1_LOADS = ((0, 2), (2, 5), (5, E))
W3_LOADS = ((0, 4), (4, E))
GATE_PIECE = 512
SUM_BANKS, TURN_BANKS, Y_BANKS = 5, 2, 1
EARLY_W3 = 3
TENSOR_PIECES = (256, 256, 256, 256, 256)
VECTOR_PIECE = 256


def tile_moe_ecr_glu_sigmoid_kernel(
    tc, xT, w1_words, w1_scales, w3_words, w3_scales, w2_words, w2_scales, gate, offs, pos1, pos2, pos3, pos4, out
):
    nc = tc.nc
    with ExitStack() as ctx:
        lists = ctx.enter_context(tc.tile_pool(name="lists", bufs=1))
        keep = ctx.enter_context(tc.tile_pool(name="keep", bufs=1))
        ring = ctx.enter_context(tc.tile_pool(name="ring", bufs=3))
        psum = ctx.enter_context(tc.psum_pool(name="psum", bufs=2))

        x_codes = keep.tile([P, T], U32, name="x_codes", align_bytes=64)
        x_scales = keep.tile([P, T], U8, name="x_scales", align_bytes=64)
        nc.gpsimd.memset(x_scales[:], 0)
        ident = keep.tile([P, P], F32, name="ident")
        make_identity(nc, ident[:])

        w1_plane = keep.tile([P, E, H], U8, name="w1_plane", align_bytes=64)
        w3_plane = keep.tile([P, E, H], U8, name="w3_plane", align_bytes=64)
        w2_plane = keep.tile([P, E, N], U8, name="w2_plane", align_bytes=64)
        for plane in (w1_plane, w3_plane, w2_plane):
            nc.vector.memset(plane[:].bitcast(I32), 0)
        y_all = keep.tile([P, S + PAD], F32, name="y_all")
        nc.vector.memset(y_all[:, S:], 0.0)

        x_rows = xT.rearrange("(p j) t -> p j t", j=PACK)
        x_raw = []
        t0 = 0
        for piece, (width, on_vector) in enumerate(X_PIECES):
            raw = keep.tile([P, PACK, width], F32, name=f"x_raw{piece}")
            nc.sync.dma_start(raw[:], x_rows[:, :, t0 : t0 + width])
            x_raw.append(raw)
            t0 += width
        offs_sb = lists.tile([P, S // PER_COL], U16, name="offs_sb")
        nc.sync.dma_start(offs_sb[:], offs)

        w1_sb = keep.tile([P, E, 2 * H], U8, name="w1_sb", align_bytes=64)
        w3_sb = keep.tile([P, E, 2 * H], U8, name="w3_sb", align_bytes=64)
        w2_sb = keep.tile([P, E, 2 * N], U8, name="w2_sb", align_bytes=64)

        def load_words(dst, src, e0, e1):
            nc.sync.dma_start(
                dst[:, e0:e1, :].bitcast(I32), src[e0:e1].rearrange("e s p c -> p (e s) c").bitcast(I32)
            )

        def load_scales(dst, src):
            rows = src.rearrange("e s q c -> q (e s) c")
            for quad in (0, 2, 1, 3):
                nc.sync.dma_start(
                    dst[32 * quad : 32 * quad + 4, :, :].bitcast(I32), rows[4 * quad : 4 * quad + 4].bitcast(I32)
                )

        load_scales(w1_plane, w1_scales)
        for e0, e1 in W1_LOADS:
            load_words(w1_sb, w1_words, e0, e1)
        load_scales(w3_plane, w3_scales)
        for e0, e1 in W3_LOADS:
            load_words(w3_sb, w3_words, e0, e1)
        load_scales(w2_plane, w2_scales)
        load_words(w2_sb, w2_words, 0, E)
        pos_sb = []
        for r, pos in enumerate((pos1, pos2, pos3, pos4)):
            pos_tile = lists.tile([P, T // PER_COL], U16, name=f"pos_sb{r}")
            nc.sync.dma_start(pos_tile[:], pos)
            pos_sb.append(pos_tile)
        gate_sb = keep.tile([P, TOP, T], F32, name="gate_sb")
        gate_rows = gate.rearrange("r p t -> p r t")
        for t0 in range(0, T, GATE_PIECE):
            nc.sync.dma_start(gate_sb[:, :, t0 : t0 + GATE_PIECE], gate_rows[:, :, t0 : t0 + GATE_PIECE])

        t0 = 0
        for piece, (width, on_vector) in enumerate(X_PIECES):
            grouped = keep.tile([P, width, PACK], BF16, name=f"x_grouped{piece}", align_bytes=64)
            nc.scalar.copy(
                grouped[:, on_vector:, :].rearrange("p (c i) j -> p c j i", i=4),
                x_raw[piece][:, :, on_vector:].rearrange("p j (c i) -> p c j i", i=4),
            )
            nc.vector.tensor_copy(
                grouped[:, :on_vector, :].rearrange("p (c i) j -> p c j i", i=4),
                x_raw[piece][:, :, :on_vector].rearrange("p j (c i) -> p c j i", i=4),
            )
            nc.vector.quantize_mx(
                x_codes[:, t0 : t0 + width].bitcast(FP8X4),
                x_scales[:, t0 : t0 + width],
                grouped[:].rearrange("p t j -> p (t j)"),
            )
            t0 += width

        slot_codes, slot_scales = {}, {}
        b_ps, sig, h_pairs = {}, {}, {}
        h_grouped, h_codes, h_scales, y_ps = {}, {}, {}, {}

        def gather_tokens(e):
            offsets = offs_sb[:, e * C // PER_COL : (e + 1) * C // PER_COL]
            slot_codes[e] = keep.tile([P, C], U32, name=f"slot_codes{e}", align_bytes=64)
            nc.vector.tensor_copy(slot_codes[e][:], x_codes[:].indirect(offsets))
            slot_scales[e] = keep.tile([P, C], U8, name=f"slot_scales{e}", align_bytes=64)
            nc.vector.tensor_copy(slot_scales[e][:], x_scales[:].indirect(offsets))

        def first_layer(blk, words, plane):
            e, half = divmod(blk, 2)
            cols = slice(half * P, (half + 1) * P)
            acc = psum.tile([P, H], F32, name="acc", tag="sums", bufs=SUM_BANKS)
            nc.tensor.matmul_mx(
                acc[:],
                lhsT=slot_codes[e][:, cols].bitcast(FP8X4),
                lhsT_scale=slot_scales[e][:, cols],
                rhs=words[:, e, :].bitcast(FP4X4),
                rhs_scale=plane[:, e, :],
                start=True,
                stop=True,
            )
            return acc

        def as_stored(tile):
            return tile[:].rearrange("s (u p v) -> s u p v", u=2, v=2)

        def as_summed(tile):
            return tile[:].rearrange("s (p u v) -> s u p v", u=2, v=2)

        def sigmoid_of_w1(blk):
            a_ps = first_layer(blk, w1_sb, w1_plane)
            sig[blk] = keep.tile([P, H], F32, name=f"sig{blk}")
            nc.scalar.activation(as_stored(sig[blk]), as_summed(a_ps), SIGMOID)

        def product_w3(blk):
            b_ps[blk] = first_layer(blk, w3_sb, w3_plane)

        def gated(blk):
            h = ring.tile([P, H], BF16, name="h", bufs=4)
            nc.vector.tensor_tensor(as_stored(h), as_summed(b_ps[blk]), as_stored(sig[blk]), MULT)
            h_pairs[blk] = h[:].bitcast(F32)

        def turn(run):
            turned = psum.tile([P, len(run), 2, P], F32, name="turned", tag="turned", bufs=TURN_BANKS)
            for b, blk in enumerate(run):
                for u in range(2):
                    nc.tensor.transpose(turned[:, b, u, :], h_pairs[blk][:, u * P : (u + 1) * P], ident[:])
            h_grouped[run] = ring.tile([P, PACK * P * len(run)], BF16, name="h_grouped", align_bytes=64, bufs=4)
            nc.scalar.copy(
                h_grouped[run][:].bitcast(F32).rearrange("p (b s u) -> p b s u", b=len(run), u=2),
                turned[:].rearrange("p b u s -> p b s u"),
            )

        def quantise_h(run):
            h_codes[run] = ring.tile([P, P * len(run)], U32, name="h_codes", align_bytes=64, bufs=4)
            h_scales[run] = ring.tile([P, P * len(run)], U8, name="h_scales", align_bytes=64, bufs=4)
            nc.vector.quantize_mx(h_codes[run][:].bitcast(FP8X4), h_scales[run][:], h_grouped[run][:])

        def second_layer(run, tag, bufs):
            e = run[0] // 2
            y_ps[run] = psum.tile([P, P * len(run)], F32, name="y_ps", tag=tag, bufs=bufs)
            nc.tensor.matmul_mx(
                y_ps[run][:],
                lhsT=w2_sb[:, e, :].bitcast(FP4X4),
                lhsT_scale=w2_plane[:, e, :],
                rhs=h_codes[run][:].bitcast(FP8X4),
                rhs_scale=h_scales[run][:],
                start=True,
                stop=True,
            )

        def copy_y(run, copy):
            copy(y_all[:, run[0] * P : (run[-1] + 1) * P], y_ps[run][:])

        def both_blocks(e):
            return (2 * e, 2 * e + 1)

        for e in range(E):
            gather_tokens(e)
            if e == E - 1:
                for blk in range(EARLY_W3):
                    product_w3(blk)
            for blk in both_blocks(e):
                sigmoid_of_w1(blk)

        next_w3 = EARLY_W3
        for blk in range(BLOCKS):
            e, half = divmod(blk, 2)
            gated(blk)
            if half == 0 and 2 <= e < E - 1:
                quantise_h(both_blocks(e - 2))
            if half == 1 and e < E - 1:
                turn(both_blocks(e))
            if half == 1 and 2 <= e < E - 1:
                second_layer(both_blocks(e - 2), "y", Y_BANKS)
                copy_y(both_blocks(e - 2), nc.scalar.copy)
            if blk == BLOCKS - 2:
                turn((blk,))
            ahead = EARLY_W3 if blk < EARLY_W3 - 1 else SUM_BANKS
            while next_w3 <= min(blk + ahead, BLOCKS - 1):
                product_w3(next_w3)
                next_w3 += 1

        last_runs = (both_blocks(E - 3), both_blocks(E - 2), (BLOCKS - 2,), (BLOCKS - 1,))
        turn(last_runs[-1])
        for run in last_runs:
            quantise_h(run)
            second_layer(run, "sums", SUM_BANKS)
        for run in last_runs[:-1]:
            copy_y(run, nc.scalar.copy)
        copy_y(last_runs[-1], nc.vector.tensor_copy)

        def weighted(r, t0, width):
            term = ring.tile([P, width], F32, name=f"term{r}")
            offsets = pos_sb[r][:, t0 // PER_COL : (t0 + width) // PER_COL]
            nc.vector.tensor_tensor(term[:], y_all[:].indirect(offsets), gate_sb[:, r, t0 : t0 + width], MULT)
            return term

        summed_sb = {}

        def add_terms(piece):
            t0, width = sum(TENSOR_PIECES[:piece]), TENSOR_PIECES[piece]
            summed = [psum.tile([P, P], F32, name="summed", tag="sums", bufs=SUM_BANKS) for b in range(width // P)]
            for r in range(TOP):
                term = weighted(r, t0, width)
                for b in range(width // P):
                    nc.tensor.matmul(
                        summed[b][:],
                        lhsT=term[:, b * P : (b + 1) * P],
                        rhs=ident[:],
                        start=(r == 0),
                        stop=(r == TOP - 1),
                        is_transpose=True,
                    )
                if r == TOP // 2 - 1 and piece >= 1:
                    turn_back(piece - 1)
            summed_sb[piece] = ring.tile([P, width], F32, name="summed_sb", bufs=2)
            for b in range(width // P):
                nc.scalar.copy(summed_sb[piece][:, b * P : (b + 1) * P], summed[b][:])

        def turn_back(piece):
            t0, width = sum(TENSOR_PIECES[:piece]), TENSOR_PIECES[piece]
            back = psum.tile([P, width], F32, name="back", tag="turned", bufs=TURN_BANKS)
            for b in range(width // P):
                nc.tensor.transpose(back[:, b * P : (b + 1) * P], summed_sb[piece][:, b * P : (b + 1) * P], ident[:])
            result = ring.tile([P, width], F32, name="result")
            nc.scalar.copy(result[:], back[:])
            nc.scalar.dma_start(out[:, t0 : t0 + width], result[:])

        for piece in range(len(TENSOR_PIECES)):
            add_terms(piece)
        turn_back(len(TENSOR_PIECES) - 1)

        t0 = T - VECTOR_PIECE
        terms = [weighted(r, t0, VECTOR_PIECE) for r in range(TOP - 1)]
        two_terms = keep.tile([P, VECTOR_PIECE], F32, name="two_terms")
        nc.vector.tensor_tensor(two_terms[:], terms[0][:], terms[1][:], ADD)
        terms.append(weighted(TOP - 1, t0, VECTOR_PIECE))
        three_terms = keep.tile([P, VECTOR_PIECE], F32, name="three_terms")
        nc.vector.tensor_tensor(three_terms[:], two_terms[:], terms[2][:], ADD)
        four_terms = keep.tile([P, VECTOR_PIECE], F32, name="four_terms")
        nc.vector.tensor_tensor(four_terms[:], three_terms[:], terms[3][:], ADD)
        nc.sync.dma_start(out[:, t0:], four_terms[:])
